import numpy as np
import ml_dtypes


def mxq(x, axis, fmt="e4m3"):
    dtype, down = {"e4m3": (ml_dtypes.float8_e4m3fn, 7), "e5m2": (ml_dtypes.float8_e5m2, 14)}[fmt]
    v = np.moveaxis(np.asarray(x, np.float32).astype(ml_dtypes.bfloat16).astype(np.float64), axis, -1)
    blocks = v.reshape(v.shape[:-1] + (-1, 32))
    amax = np.abs(blocks).max(-1, keepdims=True)
    byte = np.maximum(np.where(amax > 0, np.frexp(amax)[1] - 1 + 127, 0) - down, 1)
    scale = np.exp2(byte - 127.0)
    codes = (blocks / scale).astype(np.float32).astype(dtype).astype(np.float64)
    return np.moveaxis((codes * scale).reshape(v.shape), -1, axis)


WIDE = False


def mx_kscale(k):
    if not WIDE:
        return np.ones(k)
    levels = np.array([10, -10, 5, -5, 0])
    if k % 512:
        return np.exp2(np.random.permutation(np.resize(levels, k // 32))).repeat(32)
    a = np.empty((k // 512, 16))
    for p in range(k // 512):
        a[p, :8] = np.random.permutation(np.resize(levels, 8))
        for g in range(8):
            far = levels[np.abs(levels - a[p, g]) >= 10]
            a[p, g + 8] = far[np.random.randint(len(far))]
    return np.exp2(a.ravel()).repeat(32)


def f64(x):
    return np.asarray(x).astype(np.float64)


def striped(idx):
    return np.tile(idx.reshape(-1, 16).T, (8, 1)).astype(np.uint16)


def unstriped(offs):
    return offs[:16].T.reshape(-1).astype(np.int64)


E2M1 = np.array([0.0, 0.5, 1.0, 1.5, 2.0, 3.0, 4.0, 6.0, -0.0, -0.5, -1.0, -1.5, -2.0, -3.0, -4.0, -6.0])


def pack_weight(w, fmt):
    k, n = w.shape
    w = f64(np.asarray(w, np.float32).astype(ml_dtypes.bfloat16)).reshape(k // 32, 32, n)
    amax = np.abs(w).max(1)
    if fmt == "e4m3":
        byte = np.frexp(amax)[1] - 1 + 127 - 7
    else:
        mant, ex = np.frexp(amax / 6.0)
        byte = np.where(mant > 0.5, ex, ex - 1) + 127
    byte = np.clip(np.where(amax > 0, byte, 1), 1, 254)
    scaled = (w * np.exp2(127.0 - byte)[:, None, :]).reshape(k, n).astype(np.float32)
    by_word = np.ascontiguousarray(scaled.reshape(k // 512, 128, 4, n).transpose(0, 1, 3, 2))
    if fmt == "e4m3":
        words = by_word.astype(ml_dtypes.float8_e4m3fn).view(np.uint8)
    else:
        c = by_word.astype(ml_dtypes.float4_e2m1fn).view(np.uint8) & 0xF
        words = (c[..., 0::2] | (c[..., 1::2] << 4)).reshape(k // 512, 128, 2 * n)
    return np.ascontiguousarray(words), np.ascontiguousarray(byte.astype(np.uint8).reshape(k // 512, 16, n))


def unpack_weight(words, scales, fmt):
    g, _, n = scales.shape
    words = np.ascontiguousarray(words).reshape(g, 128, n, -1)
    if fmt == "e4m3":
        vals = words.view(ml_dtypes.float8_e4m3fn).astype(np.float64)
    else:
        nib = np.empty((g, 128, n, 4), np.uint8)
        nib[..., 0::2] = words & 0xF
        nib[..., 1::2] = words >> 4
        vals = E2M1[nib]
    vals = vals * np.repeat(np.exp2(scales.astype(np.float64) - 127.0), 8, axis=1)[..., None]
    return vals.transpose(0, 1, 3, 2).reshape(g * 512, n)


def gelu(v):
    return 0.5 * v * (1.0 + np.tanh(np.sqrt(2.0 / np.pi) * (v + 0.044715 * v**3)))


def bf(x):
    return np.asarray(x, np.float32).astype(ml_dtypes.bfloat16)


def planes(Y):
    n, m = Y.shape
    b = f64(bf(Y)).reshape(n // 32, 32, m)
    amax = np.abs(b).max(1)
    byte = np.clip(np.where(amax > 0, np.frexp(amax)[1] - 1 + 127 - 7, 1), 1, 254)
    codes = (b * np.exp2(127.0 - byte)[:, None, :]).reshape(n, m).astype(np.float32).astype(ml_dtypes.float8_e4m3fn).view(np.uint8)
    words = codes.reshape(n // 512, 128, 4, m).transpose(0, 1, 3, 2)
    return np.ascontiguousarray(words), np.ascontiguousarray(byte.astype(np.uint8).reshape(n // 512, 16, m))


K, H, T, S, T2, P = 1024, 1024, 2048, 1024, 2048, 512

def setup_inputs():
    n = np.random.standard_normal
    s = mx_kscale(K)[:, None]
    u = mx_kscale(H)[:, None]
    row = np.exp(0.4 * n(H))
    d = {}
    d["tab_words"], d["tab_scales"] = pack_weight(n((K, T)) * s, "e4m3")
    d["offs"] = striped(np.random.permutation(T)[:S])
    d["w4_words"], d["w4_scales"] = pack_weight(n((K, H)) / s / K**0.5, "e2m1")
    d["w1"] = (1.5 * n((K, H)) / s * u.T / K**0.5).astype(np.float32)
    d["page0"] = (n((H, T2)) * u).astype(np.float32)
    d["wgs"] = np.exp(0.3 * n((128, S))).astype(np.float32)
    d["offs2"] = striped(np.random.permutation(T2)[:S])
    d["offs3"] = striped(np.random.permutation(T2)[:P])
    d["offs4"] = striped(np.random.permutation(T2)[:P])
    d["steep"] = (np.random.uniform(1.2, 2.0, H) / u[:, 0]).astype(np.float32)
    d["lift"] = (np.random.uniform(0.6, 1.4, H) * u[:, 0]).astype(np.float32)
    d["w3"] = (1.4 * n((H, H)) / u * row[None, :] / H**0.5).astype(np.float32)
    d["pond"] = (np.random.uniform(0.6, 1.5, H) * row / u[:, 0]).astype(np.float32)
    return d

def reference(tab_words, tab_scales, offs, w4_words, w4_scales, w1, page0, wgs, offs2, offs3, offs4, steep, lift, w3, pond):
    v = unpack_weight(tab_words, tab_scales, "e4m3")[:, unstriped(offs)]
    w4 = unpack_weight(w4_words, w4_scales, "e2m1")
    stir = w4.T @ v
    level = mxq(f64(w1), 0, "e4m3").T @ v
    h = np.exp(-np.abs(stir)) * level
    page = f64(page0).copy()
    page[:, unstriped(offs2)] = np.tile(f64(wgs), (H // 128, 1)) * h
    x = f64(lift)[:, None] * np.tanh(f64(steep)[:, None] * page[:, unstriped(offs3)])
    boats = mxq(f64(w3), 0, "e4m3").T @ mxq(x, 0, "e4m3")
    side = f64(pond)[:, None] * page[:, unstriped(offs4)]
    y = np.maximum(boats, side) * boats
    words, scales = planes(y)
    return y, words, scales

@@ -1,0 +1,362 @@
+from contextlib import ExitStack
+
+import concourse.mybir as mybir
+from concourse.masks import make_identity
+
+K, H, T, S, T2, M = 1024, 1024, 2048, 1024, 2048, 512
+FLOPS = 2 * K * H * S * 2 + 2 * H * H * M
+
+F32 = mybir.dt.float32
+BF16 = mybir.dt.bfloat16
+I32 = mybir.dt.int32
+U32 = mybir.dt.uint32
+U16 = mybir.dt.uint16
+U8 = mybir.dt.uint8
+FP8X4 = mybir.dt.float8_e4m3fn_x4
+FP4X4 = mybir.dt.float4_e2m1fn_x4
+ACT = mybir.ActivationFunctionType
+ALU = mybir.AluOpType
+
+P = 128
+PACK = 4
+PASS = P * PACK
+BANK = 512
+QUADS = 4
+LN_TOP = 2.0**64
+LN_BOTTOM = 2.0**-64
+SMALLEST_NORMAL = 2.0**-126
+
+
+def tile_list_lock_pound_scores_kernel(
+    tc, tab_words, tab_scales, offs, w4_words, w4_scales, w1, page0, wgs, offs2, offs3, offs4,
+    steep, lift, w3, pond, out_0, out_1, out_2,
+):
+    nc = tc.nc
+    with ExitStack() as ctx:
+        lists = ctx.enter_context(tc.tile_pool(name="lists", bufs=1))
+        sb = ctx.enter_context(tc.tile_pool(name="sb", bufs=1))
+        ps = ctx.enter_context(tc.psum_pool(name="ps", bufs=2))
+
+        def sbuf(shape, dtype, name, tag=None, bufs=1):
+            return sb.tile(shape, dtype, name=name, tag=tag or name, bufs=bufs, align_bytes=64)
+
+        def bank(name, tag):
+            return ps.tile([P, BANK], F32, name=name, tag=tag)
+
+        def load_list(src, name):
+            held = lists.tile(list(src.shape), U16, name=name)
+            nc.sync.dma_start(held[:], src)
+            return held
+
+        def load_scale_rows(queue, plane, src):
+            for quad in range(QUADS):
+                queue.dma_start(
+                    plane[32 * quad : 32 * quad + 4, :, :].bitcast(I32),
+                    src[:, 4 * quad : 4 * quad + 4, :].rearrange("a r n -> r a n").bitcast(I32),
+                )
+
+        def load_weight(w, b, a, name, tag="raw", bufs=2):
+            raw = sbuf([P, PACK, BANK], F32, name, tag=tag, bufs=bufs)
+            rows = w[PASS * a : PASS * (a + 1), BANK * b : BANK * (b + 1)]
+            nc.sync.dma_start(raw[:], rows.rearrange("(p j) c -> p j c", j=PACK))
+            return raw
+
+        def round_weight(copy, raw, name, tag="rounded", bufs=3):
+            dealt = sbuf([P, PACK * BANK], BF16, name, tag=tag, bufs=bufs)
+            copy(
+                dealt[:].rearrange("p (t q j) -> p q t j", t=PACK, j=PACK),
+                raw[:].rearrange("p j (q t) -> p q t j", t=PACK),
+            )
+            return dealt
+
+        def quantize(rounded, name, tag):
+            codes = sbuf([P, BANK], U32, name + "_codes", tag=tag + "_codes")
+            scales = sbuf([P, BANK], U8, name + "_scales", tag=tag + "_scales")
+            nc.vector.quantize_mx(out=codes[:].bitcast(FP8X4), scales=scales[:], in_=rounded[:])
+            return codes, scales
+
+        def interleave(copy, dst, src):
+            copy(
+                dst.rearrange("p (c i t) -> p c t i", i=4, t=PACK),
+                src.rearrange("p t (c i) -> p c t i", i=4),
+            )
+
+        def load_page(i):
+            b, t = divmod(i, PACK)
+            page = sbuf([P, T2], F32, "page%d" % i)
+            rows = page0[PASS * b : PASS * (b + 1), :].rearrange("(p t) c -> p t c", t=PACK)
+            nc.sync.dma_start(page[:], rows[:, t, :])
+            return page
+
+        def load_column(vec, name):
+            held = sbuf([P, 2, PACK], F32, name)
+            nc.sync.dma_start(held[:], vec.rearrange("(b p t) -> p b t", b=2, t=PACK))
+            return held
+
+        def load_w4(b):
+            held = sbuf([P, 2, 2 * BANK], U8, "w4_words%d" % b)
+            src = w4_words.rearrange("a p n -> p a n")[:, :, 2 * BANK * b : 2 * BANK * (b + 1)]
+            nc.sync.dma_start(held[:].bitcast(I32), src.bitcast(I32))
+            return held
+
+        def load_table(a):
+            held = sbuf([P, T], U32, "tab_words%d" % a, tag="early%d" % a)
+            nc.sync.dma_start(held[:].bitcast(I32), tab_words[a].rearrange("p n i -> p (n i)").bitcast(I32))
+            return held
+
+        tab_plane = sbuf([P, 2, T], U8, "tab_plane", tag="late_x")
+        nc.vector.memset(tab_plane[:, 0, :].bitcast(I32), 0)
+        nc.gpsimd.memset(tab_plane[:, 1, :].bitcast(I32), 0)
+        w4_plane = sbuf([P, 2, H], U8, "w4_plane")
+        nc.vector.memset(w4_plane[:].rearrange("p a n -> p (a n)").bitcast(I32), 0)
+        ident = sbuf([P, P], F32, "ident")
+        make_identity(nc, ident[:])
+
+        idx = load_list(offs, "idx")
+        load_scale_rows(nc.scalar, tab_plane, tab_scales)
+        gains = sbuf([P, 2, S], F32, "gains", tag="ring0")
+        nc.sync.dma_start(gains[:, 0, :], wgs)
+        table = [load_table(0)]
+        table.append(load_table(1))
+        load_scale_rows(nc.sync, w4_plane, w4_scales)
+        w4 = [load_w4(0)]
+        w1_raw = {(0, 0): load_weight(w1, 0, 0, "w1_raw00"), (0, 1): load_weight(w1, 0, 1, "w1_raw01", "late_v", 1)}
+        idx2 = load_list(offs2, "idx2")
+        pages = [load_page(0), load_page(1)]
+
+        v_codes, v_scales = {}, {}
+
+        def gather_scales(a, h, tag=None):
+            v_scales[a, h] = sbuf([P, BANK], U8, "v_scales%d%d" % (a, h), tag=tag)
+            nc.vector.tensor_copy(v_scales[a, h][:], tab_plane[:, a, :].indirect(idx[:, 32 * h : 32 * (h + 1)]))
+
+        def gather_words(a, h, held):
+            v_codes[a, h] = held[:, a, :]
+            nc.vector.tensor_copy(v_codes[a, h], table[a][:].indirect(idx[:, 32 * h : 32 * (h + 1)]))
+
+        parts = sbuf([P, 2, S], F32, "gain_parts", tag="ring1")
+        whole, low, mid, high = gains[:, 0, :], gains[:, 1, :], parts[:, 0, :], parts[:, 1, :]
+        nc.vector.tensor_scalar(mid, whole, LN_BOTTOM, LN_TOP, ALU.max, ALU.min)
+        nc.vector.tensor_scalar(low, whole, SMALLEST_NORMAL, LN_BOTTOM, ALU.max, ALU.min)
+        nc.vector.tensor_scalar_max(high, whole, LN_TOP)
+        first_words = sbuf([P, 2, BANK], U32, "first_words")
+        gather_scales(0, 0)
+        gather_scales(1, 0)
+        gather_words(0, 0, first_words)
+        gather_words(1, 0, first_words)
+        gather_scales(0, 1)
+        nc.scalar.activation(mid, mid, ACT.Ln)
+        nc.scalar.activation(low, low, ACT.Ln, scale=LN_TOP)
+        nc.scalar.activation(high, high, ACT.Ln, scale=LN_BOTTOM)
+        warm = sbuf([P, 1], F32, "warm")
+        nc.scalar.activation(warm[:], high[:, 0:1], ACT.Exp)
+        log_banks = []
+        for h in range(2):
+            log_bank = bank("log_bank%d" % h, "log")
+            for n, part in enumerate((mid, low, high)):
+                for cc in range(4):
+                    c = 4 * h + cc
+                    nc.tensor.matmul(
+                        log_bank[:, P * cc : P * (cc + 1)], part[:, P * c : P * (c + 1)], ident[:],
+                        start=(n == 0 and cc == 0), stop=(n == 2 and cc == 3), is_transpose=True,
+                    )
+            log_banks.append(log_bank)
+        neg_log = {0: sbuf([P, 8, P], F32, "neg_log0")[:]}
+
+        def deal_logs(t, h):
+            src = log_banks[h][:].rearrange("p (c u t) -> p c u t", c=4, t=PACK)[:, :, :, t]
+            nc.scalar.activation(
+                neg_log[t][:, 4 * h : 4 * h + 4, :].rearrange("p c (r u) -> p c r u", r=4),
+                src.unsqueeze(2).to_broadcast([P, 4, 4, 32]),
+                ACT.Copy, scale=-1.0,
+            )
+
+        size = {}
+
+        def stir_sizes(b, h):
+            tag = ("size%d" if b == 0 else "early%d") % h
+            size[b, h] = sbuf([P, 4, PACK, P], F32, "size%d%d" % (b, h), tag=tag)
+            for cc in range(4):
+                acc = bank("stir%d%d%d" % (b, h, cc), "stir")
+                cols = slice(P * cc, P * (cc + 1))
+                for a in range(2):
+                    nc.tensor.matmul_mx(
+                        out=acc[:],
+                        lhsT=v_codes[a, h][:, cols].bitcast(FP8X4), lhsT_scale=v_scales[a, h][:, cols],
+                        rhs=w4[b][:, a, :].bitcast(FP4X4), rhs_scale=w4_plane[:, a, BANK * b : BANK * (b + 1)],
+                        start=(a == 0), stop=(a == 1),
+                    )
+                nc.scalar.activation(
+                    size[b, h][:, cc, :, :], acc[:].rearrange("p (q t) -> p t q", t=PACK), ACT.Abs
+                )
+
+        w1_mx = {}
+        ring_tags = ["ring2", "ring0", "ring1", "last"]
+
+        factors = {}
+
+        def make_factors(i, h):
+            b, t = divmod(i, PACK)
+            cols = slice(P * t, P * (t + 1))
+            if h == 0:
+                factors[i] = sbuf([P, 2, S], F32, "factors%d" % i, tag=ring_tags[i % 4])
+            half = slice(BANK * h, BANK * (h + 1))
+            arg = bank("arg%d%d" % (i, h), "arg")
+            for cc in range(4):
+                nc.tensor.matmul(
+                    arg[:, P * cc : P * (cc + 1)], neg_log[t][:, 4 * h + cc, :], ident[:],
+                    start=(cc == 0), stop=False, is_transpose=True,
+                )
+            for cc in range(4):
+                nc.tensor.matmul(
+                    arg[:, P * cc : P * (cc + 1)], size[b, h][:, cc, t, :], ident[:],
+                    start=False, stop=(cc == 3), is_transpose=True,
+                )
+            nc.scalar.activation(factors[i][:, 0, half], arg[:], ACT.Exp, scale=-1.0)
+            level = bank("level%d%d" % (i, h), "level")
+            for a in range(2):
+                codes, scales = w1_mx[b, a]
+                nc.tensor.matmul_mx(
+                    out=level[:],
+                    lhsT=codes[:, cols].bitcast(FP8X4), lhsT_scale=scales[:, cols],
+                    rhs=v_codes[a, h].bitcast(FP8X4), rhs_scale=v_scales[a, h][:],
+                    start=(a == 0), stop=(a == 1),
+                )
+            nc.scalar.copy(factors[i][:, 1, half], level[:])
+
+        def scatter(i, first, count):
+            cols = slice(first, first + count)
+            nc.vector.tensor_tensor(
+                pages[i][:].indirect(idx2[:, first // 16 : (first + count) // 16]),
+                factors[i][:, 0, cols], factors[i][:, 1, cols], ALU.mult,
+            )
+
+        def refresh(i):
+            make_factors(i, 0)
+            make_factors(i, 1)
+            scatter(i, 0, S)
+
+        for h in range(2):
+            deal_logs(0, h)
+        stir_sizes(0, 0)
+        rounded = round_weight(nc.vector.tensor_copy, w1_raw[0, 0], "w1_bf00", "late_scales", 1)
+        w1_mx[0, 0] = quantize(rounded, "w1_00", "w1_00")
+        rounded = round_weight(nc.vector.tensor_copy, w1_raw[0, 1], "w1_bf01", "late_logs", 1)
+        w1_mx[0, 1] = quantize(rounded, "w1_01", "w1_01")
+        second_words = sbuf([P, 2, BANK], U32, "second_words", tag="late_v")
+        gather_scales(1, 1, "late_scales")
+        gather_words(0, 1, second_words)
+        gather_words(1, 1, second_words)
+        late_logs = sbuf([P, 3, 8, P], F32, "late_logs")
+        for t in range(1, PACK):
+            neg_log[t] = late_logs[:, t - 1, :, :]
+        make_factors(0, 0)
+        scatter(0, 0, BANK)
+        stir_sizes(0, 1)
+        deal_logs(1, 0)
+        make_factors(1, 0)
+        make_factors(0, 1)
+        scatter(1, 0, BANK)
+        scatter(0, BANK, BANK)
+        deal_logs(1, 1)
+        make_factors(1, 1)
+        scatter(1, BANK, BANK)
+        for t in range(2, PACK):
+            for h in range(2):
+                deal_logs(t, h)
+
+        w1_raw[1, 0] = load_weight(w1, 1, 0, "w1_raw10")
+        w1_raw[1, 1] = load_weight(w1, 1, 1, "w1_raw11")
+        w4.append(load_w4(1))
+        pages.append(load_page(2))
+        for a in range(2):
+            rounded = round_weight(nc.scalar.copy, w1_raw[1, a], "w1_bf1%d" % a)
+            w1_mx[1, a] = quantize(rounded, "w1_1%d" % a, "w1_1%d" % a)
+        refresh(2)
+        pages.append(load_page(3))
+        stir_sizes(1, 0)
+        refresh(3)
+        stir_sizes(1, 1)
+        idx3 = load_list(offs3, "idx3")
+        idx4 = load_list(offs4, "idx4")
+        steep_col = load_column(steep, "steep_col")
+        lift_col = load_column(lift, "lift_col")
+        pond_col = load_column(pond, "pond_col")
+        w3_mx = {}
+        for n in range(4):
+            g, a = divmod(n, 2)
+            raw = load_weight(w3, g, a, "w3_raw%d%d" % (g, a))
+            rounded = round_weight(nc.scalar.copy, raw, "w3_bf%d%d" % (g, a))
+            w3_mx[g, a] = quantize(rounded, "w3_%d%d" % (g, a), "w3_%d%d" % (g, a))
+        for i in range(4, 8):
+            pages.append(load_page(i))
+            refresh(i)
+
+        picked = sbuf([P, 8, M], F32, "picked", tag="last")
+        x_mx = []
+        bounded = [sbuf([P, PACK, M], F32, "bounded%d" % b, tag="size%d" % b) for b in range(2)]
+        for i in range(8):
+            nc.vector.tensor_copy(picked[:, i, :], pages[i][:].indirect(idx3[:]))
+        for b in range(2):
+            for t in range(PACK):
+                i = PACK * b + t
+                nc.scalar.activation(bounded[b][:, t, :], picked[:, i, :], ACT.Tanh, scale=steep_col[:, b, t : t + 1])
+                nc.scalar.activation(bounded[b][:, t, :], bounded[b][:, t, :], ACT.Copy, scale=lift_col[:, b, t : t + 1])
+            if b == 0:
+                x_bf = sbuf([P, PACK * M], BF16, "x_bf0", tag="rounded", bufs=3)
+            else:
+                x_bf = sbuf([P, PACK * M], BF16, "x_bf1", tag="late_x")
+            interleave(nc.scalar.copy, x_bf[:], bounded[b][:])
+            x_mx.append(quantize(x_bf, "x%d" % b, "w1_0%d" % b))
+        side_late = sbuf([P, 2, M], F32, "side_late", tag="late_x")
+        side = [picked[:, i, :] if i < 6 else side_late[:, i - 6, :] for i in range(8)]
+        for i in range(8):
+            nc.vector.tensor_copy(side[i], pages[i][:].indirect(idx4[:]))
+
+        boats = [bank("boats%d" % i, ("log", "stir", "arg", "level")[i // 2]) for i in range(8)]
+        for a in range(2):
+            for i in range(8):
+                g, t = divmod(i, PACK)
+                cols = slice(P * t, P * (t + 1))
+                codes, scales = w3_mx[g, a]
+                nc.tensor.matmul_mx(
+                    out=boats[i][:],
+                    lhsT=codes[:, cols].bitcast(FP8X4), lhsT_scale=scales[:, cols],
+                    rhs=x_mx[a][0][:].bitcast(FP8X4), rhs_scale=x_mx[a][1][:],
+                    start=(a == 0), stop=(a == 1),
+                )
+
+        y_codes = sbuf([P, 2, M], U32, "y_codes")
+        y_scales = sbuf([P, 2, M], U8, "y_scales")
+        out_rows = out_0.rearrange("(g p t) m -> g p t m", g=2, t=PACK)
+        for g in range(2):
+            y = sbuf([P, PACK, M], F32, "y%d" % g, tag="raw", bufs=2)
+            y_bf = sbuf([P, PACK * M], BF16, "y_bf%d" % g, tag="rounded", bufs=3)
+            larger = sbuf([P, PACK, M], F32, "larger%d" % g, tag="ring%d" % g)
+            pieces = 1 + g
+            width = M // pieces
+            for n in range(pieces):
+                cols = slice(width * n, width * (n + 1))
+                for t in range(PACK):
+                    i = PACK * g + t
+                    nc.vector.scalar_tensor_tensor(
+                        larger[:, t, cols], side[i][:, cols], pond_col[:, g, t : t + 1], boats[i][:, cols],
+                        ALU.mult, ALU.max,
+                    )
+                for t in range(PACK):
+                    i = PACK * g + t
+                    nc.vector.tensor_tensor(y[:, t, cols], larger[:, t, cols], boats[i][:, cols], ALU.mult)
+                nc.sync.dma_start(out_rows[g][:, :, cols], y[:, :, cols])
+                last = g == 1 and n == pieces - 1
+                wide = slice(PACK * width * n, PACK * width * (n + 1))
+                interleave(nc.vector.tensor_copy if last else nc.scalar.copy, y_bf[:, wide], y[:, :, cols])
+                nc.vector.quantize_mx(
+                    out=y_codes[:, g, cols].bitcast(FP8X4), scales=y_scales[:, g, cols], in_=y_bf[:, wide]
+                )
+                words = out_1[g].rearrange("p m t -> p (m t)").bitcast(I32)
+                nc.sync.dma_start(words[:, cols], y_codes[:, g, cols].bitcast(I32))
+        for quad in range(QUADS):
+            nc.scalar.dma_start(
+                out_2[:, 4 * quad : 4 * quad + 4, :].rearrange("g r m -> r g m").bitcast(I32),
+                y_scales[32 * quad : 32 * quad + 4, :, :].bitcast(I32),
+            )

@@ -25,6 +25,7 @@ QUADS = 4
 LN_TOP = 2.0**64
 LN_BOTTOM = 2.0**-64
 SMALLEST_NORMAL = 2.0**-126
+BANKS = {"log": 1, "stir": 3, "arg": 2, "level": 2}
 
 
 def tile_list_lock_pound_scores_kernel(
@@ -41,7 +42,7 @@ def tile_list_lock_pound_scores_kernel(
             return sb.tile(shape, dtype, name=name, tag=tag or name, bufs=bufs, align_bytes=64)
 
         def bank(name, tag):
-            return ps.tile([P, BANK], F32, name=name, tag=tag)
+            return ps.tile([P, BANK], F32, name=name, tag=tag, bufs=BANKS[tag])
 
         def load_list(src, name):
             held = lists.tile(list(src.shape), U16, name=name)
@@ -61,7 +62,7 @@ def tile_list_lock_pound_scores_kernel(
             nc.sync.dma_start(raw[:], rows.rearrange("(p j) c -> p j c", j=PACK))
             return raw
 
-        def round_weight(copy, raw, name, tag="rounded", bufs=3):
+        def round_weight(copy, raw, name, tag="rounded", bufs=4):
             dealt = sbuf([P, PACK * BANK], BF16, name, tag=tag, bufs=bufs)
             copy(
                 dealt[:].rearrange("p (t q j) -> p q t j", t=PACK, j=PACK),
@@ -117,9 +118,9 @@ def tile_list_lock_pound_scores_kernel(
         gains = sbuf([P, 2, S], F32, "gains", tag="ring0")
         nc.sync.dma_start(gains[:, 0, :], wgs)
         table = [load_table(0)]
+        w4 = [load_w4(0)]
         table.append(load_table(1))
         load_scale_rows(nc.sync, w4_plane, w4_scales)
-        w4 = [load_w4(0)]
         w1_raw = {(0, 0): load_weight(w1, 0, 0, "w1_raw00"), (0, 1): load_weight(w1, 0, 1, "w1_raw01", "late_v", 1)}
         idx2 = load_list(offs2, "idx2")
         pages = [load_page(0), load_page(1)]
@@ -151,8 +152,9 @@ def tile_list_lock_pound_scores_kernel(
         warm = sbuf([P, 1], F32, "warm")
         nc.scalar.activation(warm[:], high[:, 0:1], ACT.Exp)
         log_banks = []
-        for h in range(2):
-            log_bank = bank("log_bank%d" % h, "log")
+
+        def turn_logs(h):
+            log_bank = bank("log_bank%d" % h, ("log", "stir")[h])
             for n, part in enumerate((mid, low, high)):
                 for cc in range(4):
                     c = 4 * h + cc
@@ -161,6 +163,8 @@ def tile_list_lock_pound_scores_kernel(
                         start=(n == 0 and cc == 0), stop=(n == 2 and cc == 3), is_transpose=True,
                     )
             log_banks.append(log_bank)
+
+        turn_logs(0)
         neg_log = {0: sbuf([P, 8, P], F32, "neg_log0")[:]}
 
         def deal_logs(t, h):
@@ -236,9 +240,9 @@ def tile_list_lock_pound_scores_kernel(
             make_factors(i, 1)
             scatter(i, 0, S)
 
-        for h in range(2):
-            deal_logs(0, h)
+        deal_logs(0, 0)
         stir_sizes(0, 0)
+        turn_logs(1)
         rounded = round_weight(nc.vector.tensor_copy, w1_raw[0, 0], "w1_bf00", "late_scales", 1)
         w1_mx[0, 0] = quantize(rounded, "w1_00", "w1_00")
         rounded = round_weight(nc.vector.tensor_copy, w1_raw[0, 1], "w1_bf01", "late_logs", 1)
@@ -250,70 +254,74 @@ def tile_list_lock_pound_scores_kernel(
         late_logs = sbuf([P, 3, 8, P], F32, "late_logs")
         for t in range(1, PACK):
             neg_log[t] = late_logs[:, t - 1, :, :]
-        make_factors(0, 0)
-        scatter(0, 0, BANK)
-        stir_sizes(0, 1)
-        deal_logs(1, 0)
-        make_factors(1, 0)
-        make_factors(0, 1)
-        scatter(1, 0, BANK)
-        scatter(0, BANK, BANK)
-        deal_logs(1, 1)
-        make_factors(1, 1)
-        scatter(1, BANK, BANK)
-        for t in range(2, PACK):
-            for h in range(2):
-                deal_logs(t, h)
-
         w1_raw[1, 0] = load_weight(w1, 1, 0, "w1_raw10")
         w1_raw[1, 1] = load_weight(w1, 1, 1, "w1_raw11")
-        w4.append(load_w4(1))
         pages.append(load_page(2))
-        for a in range(2):
-            rounded = round_weight(nc.scalar.copy, w1_raw[1, a], "w1_bf1%d" % a)
-            w1_mx[1, a] = quantize(rounded, "w1_1%d" % a, "w1_1%d" % a)
-        refresh(2)
-        pages.append(load_page(3))
-        stir_sizes(1, 0)
-        refresh(3)
-        stir_sizes(1, 1)
+        w4.append(load_w4(1))
+        for i in range(3, 8):
+            pages.append(load_page(i))
         idx3 = load_list(offs3, "idx3")
         idx4 = load_list(offs4, "idx4")
         steep_col = load_column(steep, "steep_col")
         lift_col = load_column(lift, "lift_col")
         pond_col = load_column(pond, "pond_col")
+        w3_raw = [load_weight(w3, 0, a, "w3_raw0%d" % a) for a in range(2)]
+
+        make_factors(0, 0)
+        scatter(0, 0, BANK)
+        stir_sizes(0, 1)
+        deal_logs(0, 1)
+        for i in (1, 2):
+            deal_logs(i, 0)
+            make_factors(i, 0)
+            scatter(i, 0, BANK)
+        for i in range(3):
+            if i > 0:
+                deal_logs(i, 1)
+            make_factors(i, 1)
+            scatter(i, BANK, BANK)
+        for a in range(2):
+            rounded = round_weight(nc.scalar.copy, w1_raw[1, a], "w1_bf1%d" % a)
+            w1_mx[1, a] = quantize(rounded, "w1_1%d" % a, "w1_1%d" % a)
+        for h in range(2):
+            deal_logs(3, h)
+        refresh(3)
+        w3_raw.extend(load_weight(w3, 1, a, "w3_raw1%d" % a, "size%d" % a, 1) for a in range(2))
+        stir_sizes(1, 0)
+        stir_sizes(1, 1)
+        refresh(4)
+        refresh(5)
         w3_mx = {}
         for n in range(4):
             g, a = divmod(n, 2)
-            raw = load_weight(w3, g, a, "w3_raw%d%d" % (g, a))
-            rounded = round_weight(nc.scalar.copy, raw, "w3_bf%d%d" % (g, a))
+            rounded = round_weight(nc.scalar.copy, w3_raw[n], "w3_bf%d%d" % (g, a))
             w3_mx[g, a] = quantize(rounded, "w3_%d%d" % (g, a), "w3_%d%d" % (g, a))
-        for i in range(4, 8):
-            pages.append(load_page(i))
-            refresh(i)
+        refresh(6)
 
-        picked = sbuf([P, 8, M], F32, "picked", tag="last")
         x_mx = []
-        bounded = [sbuf([P, PACK, M], F32, "bounded%d" % b, tag="size%d" % b) for b in range(2)]
-        for i in range(8):
-            nc.vector.tensor_copy(picked[:, i, :], pages[i][:].indirect(idx3[:]))
-        for b in range(2):
+
+        def make_x(b, picked, x_bf):
+            bounded = sbuf([P, PACK, M], F32, "bounded%d" % b, tag="size%d" % b)
             for t in range(PACK):
-                i = PACK * b + t
-                nc.scalar.activation(bounded[b][:, t, :], picked[:, i, :], ACT.Tanh, scale=steep_col[:, b, t : t + 1])
-                nc.scalar.activation(bounded[b][:, t, :], bounded[b][:, t, :], ACT.Copy, scale=lift_col[:, b, t : t + 1])
-            if b == 0:
-                x_bf = sbuf([P, PACK * M], BF16, "x_bf0", tag="rounded", bufs=3)
-            else:
-                x_bf = sbuf([P, PACK * M], BF16, "x_bf1", tag="late_x")
-            interleave(nc.scalar.copy, x_bf[:], bounded[b][:])
+                nc.vector.tensor_copy(picked[:, t, :], pages[PACK * b + t][:].indirect(idx3[:]))
+            for t in range(PACK):
+                nc.scalar.activation(bounded[:, t, :], picked[:, t, :], ACT.Tanh, scale=steep_col[:, b, t : t + 1])
+                nc.scalar.activation(bounded[:, t, :], bounded[:, t, :], ACT.Copy, scale=lift_col[:, b, t : t + 1])
+            interleave(nc.scalar.copy, x_bf[:], bounded[:])
             x_mx.append(quantize(x_bf, "x%d" % b, "w1_0%d" % b))
+
+        first_picked = sbuf([P, PACK, M], F32, "first_picked", tag=ring_tags[6 % 4])
+        refresh(7)
+        make_x(0, first_picked, sbuf([P, PACK * M], BF16, "x_bf0", tag="rounded", bufs=4))
+        picked = sbuf([P, 8, M], F32, "picked", tag="last")
+        make_x(1, picked, sbuf([P, PACK * M], BF16, "x_bf1", tag="late_x"))
         side_late = sbuf([P, 2, M], F32, "side_late", tag="late_x")
-        side = [picked[:, i, :] if i < 6 else side_late[:, i - 6, :] for i in range(8)]
+        side = [picked[:, (i + 4) % 8, :] if i < 6 else side_late[:, i - 6, :] for i in range(8)]
         for i in range(8):
             nc.vector.tensor_copy(side[i], pages[i][:].indirect(idx4[:]))
 
-        boats = [bank("boats%d" % i, ("log", "stir", "arg", "level")[i // 2]) for i in range(8)]
+        boat_tags = [tag for tag in BANKS for n in range(BANKS[tag])]
+        boats = [bank("boats%d" % i, boat_tags[i]) for i in range(8)]
         for a in range(2):
             for i in range(8):
                 g, t = divmod(i, PACK)
@@ -331,7 +339,7 @@ def tile_list_lock_pound_scores_kernel(
         out_rows = out_0.rearrange("(g p t) m -> g p t m", g=2, t=PACK)
         for g in range(2):
             y = sbuf([P, PACK, M], F32, "y%d" % g, tag="raw", bufs=2)
-            y_bf = sbuf([P, PACK * M], BF16, "y_bf%d" % g, tag="rounded", bufs=3)
+            y_bf = sbuf([P, PACK * M], BF16, "y_bf%d" % g, tag="rounded", bufs=4)
             larger = sbuf([P, PACK, M], F32, "larger%d" % g, tag="ring%d" % g)
             pieces = 1 + g
             width = M // pieces

@@ -65,8 +65,8 @@ def tile_list_lock_pound_scores_kernel(
         def round_weight(copy, raw, name, tag="rounded", bufs=4):
             dealt = sbuf([P, PACK * BANK], BF16, name, tag=tag, bufs=bufs)
             copy(
-                dealt[:].rearrange("p (t q j) -> p q t j", t=PACK, j=PACK),
-                raw[:].rearrange("p j (q t) -> p q t j", t=PACK),
+                dealt[:].rearrange("p (u e q j) -> p u q j e", u=2, e=2, j=PACK),
+                raw[:].rearrange("p j (q u e) -> p u q j e", u=2, e=2),
             )
             return dealt
 
@@ -78,8 +78,8 @@ def tile_list_lock_pound_scores_kernel(
 
         def interleave(copy, dst, src):
             copy(
-                dst.rearrange("p (c i t) -> p c t i", i=4, t=PACK),
-                src.rearrange("p t (c i) -> p c t i", i=4),
+                dst.rearrange("p (c i t) -> p c t i", i=2, t=PACK),
+                src.rearrange("p t (c i) -> p c t i", i=2),
             )
 
         def load_page(i):
@@ -291,12 +291,14 @@ def tile_list_lock_pound_scores_kernel(
         stir_sizes(1, 1)
         refresh(4)
         refresh(5)
+        refresh(6)
+        first_picked = sbuf([P, PACK, M], F32, "first_picked", tag=ring_tags[6 % 4])
+        refresh(7)
         w3_mx = {}
         for n in range(4):
             g, a = divmod(n, 2)
             rounded = round_weight(nc.scalar.copy, w3_raw[n], "w3_bf%d%d" % (g, a))
             w3_mx[g, a] = quantize(rounded, "w3_%d%d" % (g, a), "w3_%d%d" % (g, a))
-        refresh(6)
 
         x_mx = []
 
@@ -310,9 +312,7 @@ def tile_list_lock_pound_scores_kernel(
             interleave(nc.scalar.copy, x_bf[:], bounded[:])
             x_mx.append(quantize(x_bf, "x%d" % b, "w1_0%d" % b))
 
-        first_picked = sbuf([P, PACK, M], F32, "first_picked", tag=ring_tags[6 % 4])
-        refresh(7)
-        make_x(0, first_picked, sbuf([P, PACK * M], BF16, "x_bf0", tag="rounded", bufs=4))
+        make_x(0, first_picked, sbuf([P, PACK * M], BF16, "x_bf0", tag="early0"))
         picked = sbuf([P, 8, M], F32, "picked", tag="last")
         make_x(1, picked, sbuf([P, PACK * M], BF16, "x_bf1", tag="late_x"))
         side_late = sbuf([P, 2, M], F32, "side_late", tag="late_x")

@@ -62,19 +62,33 @@ def tile_list_lock_pound_scores_kernel(
             nc.sync.dma_start(raw[:], rows.rearrange("(p j) c -> p j c", j=PACK))
             return raw
 
-        def round_weight(copy, raw, name, tag="rounded", bufs=4):
-            dealt = sbuf([P, PACK * BANK], BF16, name, tag=tag, bufs=bufs)
+        def round_pairs(copy, dealt, raw, pairs):
             copy(
-                dealt[:].rearrange("p (u e q j) -> p u q j e", u=2, e=2, j=PACK),
-                raw[:].rearrange("p j (q u e) -> p u q j e", u=2, e=2),
+                dealt[:].rearrange("p (u e q j) -> p u q j e", u=2, e=2, j=PACK)[:, pairs],
+                raw[:].rearrange("p j (q u e) -> p u q j e", u=2, e=2)[:, pairs],
             )
+
+        def round_weight(copy, raw, name, tag="rounded", bufs=3):
+            dealt = sbuf([P, PACK * BANK], BF16, name, tag=tag, bufs=bufs)
+            round_pairs(copy, dealt, raw, slice(0, 2))
             return dealt
 
-        def quantize(rounded, name, tag):
+        def mx_tiles(name, tag):
             codes = sbuf([P, BANK], U32, name + "_codes", tag=tag + "_codes")
             scales = sbuf([P, BANK], U8, name + "_scales", tag=tag + "_scales")
-            nc.vector.quantize_mx(out=codes[:].bitcast(FP8X4), scales=scales[:], in_=rounded[:])
             return codes, scales
+
+        def quantize_into(mx, rounded, first, count):
+            cols = slice(first, first + count)
+            nc.vector.quantize_mx(
+                out=mx[0][:, cols].bitcast(FP8X4), scales=mx[1][:, cols],
+                in_=rounded[:, PACK * first : PACK * (first + count)],
+            )
+
+        def quantize(rounded, name, tag):
+            mx = mx_tiles(name, tag)
+            quantize_into(mx, rounded, 0, BANK)
+            return mx
 
         def interleave(copy, dst, src):
             copy(
@@ -132,7 +146,7 @@ def tile_list_lock_pound_scores_kernel(
             nc.vector.tensor_copy(v_scales[a, h][:], tab_plane[:, a, :].indirect(idx[:, 32 * h : 32 * (h + 1)]))
 
         def gather_words(a, h, held):
-            v_codes[a, h] = held[:, a, :]
+            v_codes[a, h] = held
             nc.vector.tensor_copy(v_codes[a, h], table[a][:].indirect(idx[:, 32 * h : 32 * (h + 1)]))
 
         parts = sbuf([P, 2, S], F32, "gain_parts", tag="ring1")
@@ -143,8 +157,8 @@ def tile_list_lock_pound_scores_kernel(
         first_words = sbuf([P, 2, BANK], U32, "first_words")
         gather_scales(0, 0)
         gather_scales(1, 0)
-        gather_words(0, 0, first_words)
-        gather_words(1, 0, first_words)
+        gather_words(0, 0, first_words[:, 0, :])
+        gather_words(1, 0, first_words[:, 1, :])
         gather_scales(0, 1)
         nc.scalar.activation(mid, mid, ACT.Ln)
         nc.scalar.activation(low, low, ACT.Ln, scale=LN_TOP)
@@ -249,19 +263,19 @@ def tile_list_lock_pound_scores_kernel(
         w1_mx[0, 1] = quantize(rounded, "w1_01", "w1_01")
         second_words = sbuf([P, 2, BANK], U32, "second_words", tag="late_v")
         gather_scales(1, 1, "late_scales")
-        gather_words(0, 1, second_words)
-        gather_words(1, 1, second_words)
+        gather_words(0, 1, second_words[:, 0, :])
+        gather_words(1, 1, second_words[:, 1, :])
         late_logs = sbuf([P, 3, 8, P], F32, "late_logs")
         for t in range(1, PACK):
             neg_log[t] = late_logs[:, t - 1, :, :]
         w1_raw[1, 0] = load_weight(w1, 1, 0, "w1_raw10")
         w1_raw[1, 1] = load_weight(w1, 1, 1, "w1_raw11")
         pages.append(load_page(2))
+        idx4 = load_list(offs4, "idx4")
         w4.append(load_w4(1))
         for i in range(3, 8):
             pages.append(load_page(i))
         idx3 = load_list(offs3, "idx3")
-        idx4 = load_list(offs4, "idx4")
         steep_col = load_column(steep, "steep_col")
         lift_col = load_column(lift, "lift_col")
         pond_col = load_column(pond, "pond_col")
@@ -280,16 +294,28 @@ def tile_list_lock_pound_scores_kernel(
                 deal_logs(i, 1)
             make_factors(i, 1)
             scatter(i, BANK, BANK)
+        w1_bf = [sbuf([P, PACK * BANK], BF16, "w1_bf1%d" % a, tag="rounded", bufs=3) for a in range(2)]
         for a in range(2):
-            rounded = round_weight(nc.scalar.copy, w1_raw[1, a], "w1_bf1%d" % a)
-            w1_mx[1, a] = quantize(rounded, "w1_1%d" % a, "w1_1%d" % a)
+            w1_mx[1, a] = mx_tiles("w1_1%d" % a, "w1_1%d" % a)
+
+        def quantize_pair(u):
+            for a in range(2):
+                round_pairs(nc.scalar.copy, w1_bf[a], w1_raw[1, a], slice(u, u + 1))
+                quantize_into(w1_mx[1, a], w1_bf[a], 2 * P * u, 2 * P)
+
+        quantize_pair(0)
         for h in range(2):
             deal_logs(3, h)
         refresh(3)
         w3_raw.extend(load_weight(w3, 1, a, "w3_raw1%d" % a, "size%d" % a, 1) for a in range(2))
-        stir_sizes(1, 0)
-        stir_sizes(1, 1)
-        refresh(4)
+        side_early = sbuf([P, 3, M], F32, "side_early")
+        for i in range(3):
+            nc.vector.tensor_copy(side_early[:, i, :], pages[i][:].indirect(idx4[:]))
+        for h in range(2):
+            stir_sizes(1, h)
+            make_factors(4, h)
+            scatter(4, BANK * h, BANK)
+        quantize_pair(1)
         refresh(5)
         refresh(6)
         first_picked = sbuf([P, PACK, M], F32, "first_picked", tag=ring_tags[6 % 4])
@@ -297,7 +323,8 @@ def tile_list_lock_pound_scores_kernel(
         w3_mx = {}
         for n in range(4):
             g, a = divmod(n, 2)
-            rounded = round_weight(nc.scalar.copy, w3_raw[n], "w3_bf%d%d" % (g, a))
+            place = ("rounded", 3) if n < 3 else ("early1", 1)
+            rounded = round_weight(nc.scalar.copy, w3_raw[n], "w3_bf%d%d" % (g, a), *place)
             w3_mx[g, a] = quantize(rounded, "w3_%d%d" % (g, a), "w3_%d%d" % (g, a))
 
         x_mx = []
@@ -313,11 +340,12 @@ def tile_list_lock_pound_scores_kernel(
             x_mx.append(quantize(x_bf, "x%d" % b, "w1_0%d" % b))
 
         make_x(0, first_picked, sbuf([P, PACK * M], BF16, "x_bf0", tag="early0"))
-        picked = sbuf([P, 8, M], F32, "picked", tag="last")
+        picked = sbuf([P, 5, M], F32, "picked", tag="last")
         make_x(1, picked, sbuf([P, PACK * M], BF16, "x_bf1", tag="late_x"))
         side_late = sbuf([P, 2, M], F32, "side_late", tag="late_x")
-        side = [picked[:, (i + 4) % 8, :] if i < 6 else side_late[:, i - 6, :] for i in range(8)]
-        for i in range(8):
+        side = [side_early[:, i, :] for i in range(3)]
+        side.extend([picked[:, 4, :], picked[:, 0, :], picked[:, 1, :], side_late[:, 0, :], side_late[:, 1, :]])
+        for i in range(3, 8):
             nc.vector.tensor_copy(side[i], pages[i][:].indirect(idx4[:]))
 
         boat_tags = [tag for tag in BANKS for n in range(BANKS[tag])]
@@ -339,7 +367,7 @@ def tile_list_lock_pound_scores_kernel(
         out_rows = out_0.rearrange("(g p t) m -> g p t m", g=2, t=PACK)
         for g in range(2):
             y = sbuf([P, PACK, M], F32, "y%d" % g, tag="raw", bufs=2)
-            y_bf = sbuf([P, PACK * M], BF16, "y_bf%d" % g, tag="rounded", bufs=4)
+            y_bf = sbuf([P, PACK * M], BF16, "y_bf%d" % g, tag="rounded", bufs=3)
             larger = sbuf([P, PACK, M], F32, "larger%d" % g, tag="ring%d" % g)
             pieces = 1 + g
             width = M // pieces

from contextlib import ExitStack

import concourse.mybir as mybir
from concourse.masks import make_identity

K, H, T, S, T2, M = 1024, 1024, 2048, 1024, 2048, 512
FLOPS = 2 * K * H * S * 2 + 2 * H * H * M

F32 = mybir.dt.float32
BF16 = mybir.dt.bfloat16
I32 = mybir.dt.int32
U32 = mybir.dt.uint32
U16 = mybir.dt.uint16
U8 = mybir.dt.uint8
FP8X4 = mybir.dt.float8_e4m3fn_x4
FP4X4 = mybir.dt.float4_e2m1fn_x4
ACT = mybir.ActivationFunctionType
ALU = mybir.AluOpType

P = 128
PACK = 4
PASS = P * PACK
BANK = 512
QUADS = 4
LN_TOP = 2.0**64
LN_BOTTOM = 2.0**-64
SMALLEST_NORMAL = 2.0**-126
BANKS = {"log": 1, "stir": 3, "arg": 2, "level": 2}


def tile_list_lock_pound_scores_kernel(
    tc, tab_words, tab_scales, offs, w4_words, w4_scales, w1, page0, wgs, offs2, offs3, offs4,
    steep, lift, w3, pond, out_0, out_1, out_2,
):
    nc = tc.nc
    with ExitStack() as ctx:
        lists = ctx.enter_context(tc.tile_pool(name="lists", bufs=1))
        sb = ctx.enter_context(tc.tile_pool(name="sb", bufs=1))
        ps = ctx.enter_context(tc.psum_pool(name="ps", bufs=2))

        def sbuf(shape, dtype, name, tag=None, bufs=1):
            return sb.tile(shape, dtype, name=name, tag=tag or name, bufs=bufs, align_bytes=64)

        def bank(name, tag):
            return ps.tile([P, BANK], F32, name=name, tag=tag, bufs=BANKS[tag])

        def load_list(src, name):
            held = lists.tile(list(src.shape), U16, name=name)
            nc.sync.dma_start(held[:], src)
            return held

        def load_scale_rows(queue, plane, src):
            for quad in range(QUADS):
                queue.dma_start(
                    plane[32 * quad : 32 * quad + 4, :, :].bitcast(I32),
                    src[:, 4 * quad : 4 * quad + 4, :].rearrange("a r n -> r a n").bitcast(I32),
                )

        def load_weight(w, b, a, name, tag="raw", bufs=2):
            raw = sbuf([P, PACK, BANK], F32, name, tag=tag, bufs=bufs)
            rows = w[PASS * a : PASS * (a + 1), BANK * b : BANK * (b + 1)]
            nc.sync.dma_start(raw[:], rows.rearrange("(p j) c -> p j c", j=PACK))
            return raw

        def round_pairs(copy, dealt, raw, pairs):
            copy(
                dealt[:].rearrange("p (u e q j) -> p u q j e", u=2, e=2, j=PACK)[:, pairs],
                raw[:].rearrange("p j (q u e) -> p u q j e", u=2, e=2)[:, pairs],
            )

        def round_weight(copy, raw, name, tag="rounded", bufs=3):
            dealt = sbuf([P, PACK * BANK], BF16, name, tag=tag, bufs=bufs)
            round_pairs(copy, dealt, raw, slice(0, 2))
            return dealt

        def mx_tiles(name, tag):
            codes = sbuf([P, BANK], U32, name + "_codes", tag=tag + "_codes")
            scales = sbuf([P, BANK], U8, name + "_scales", tag=tag + "_scales")
            return codes, scales

        def quantize_into(mx, rounded, first, count):
            cols = slice(first, first + count)
            nc.vector.quantize_mx(
                out=mx[0][:, cols].bitcast(FP8X4), scales=mx[1][:, cols],
                in_=rounded[:, PACK * first : PACK * (first + count)],
            )

        def quantize(rounded, name, tag):
            mx = mx_tiles(name, tag)
            quantize_into(mx, rounded, 0, BANK)
            return mx

        def interleave(copy, dst, src):
            copy(
                dst.rearrange("p (c i t) -> p c t i", i=2, t=PACK),
                src.rearrange("p t (c i) -> p c t i", i=2),
            )

        def load_page(i):
            b, t = divmod(i, PACK)
            page = sbuf([P, T2], F32, "page%d" % i)
            rows = page0[PASS * b : PASS * (b + 1), :].rearrange("(p t) c -> p t c", t=PACK)
            nc.sync.dma_start(page[:], rows[:, t, :])
            return page

        def load_column(vec, name):
            held = sbuf([P, 2, PACK], F32, name)
            nc.sync.dma_start(held[:], vec.rearrange("(b p t) -> p b t", b=2, t=PACK))
            return held

        def load_w4(b):
            held = sbuf([P, 2, 2 * BANK], U8, "w4_words%d" % b)
            src = w4_words.rearrange("a p n -> p a n")[:, :, 2 * BANK * b : 2 * BANK * (b + 1)]
            nc.sync.dma_start(held[:].bitcast(I32), src.bitcast(I32))
            return held

        def load_table(a):
            held = sbuf([P, T], U32, "tab_words%d" % a, tag="early%d" % a)
            nc.sync.dma_start(held[:].bitcast(I32), tab_words[a].rearrange("p n i -> p (n i)").bitcast(I32))
            return held

        tab_plane = sbuf([P, 2, T], U8, "tab_plane", tag="late_x")
        nc.vector.memset(tab_plane[:, 0, :].bitcast(I32), 0)
        nc.gpsimd.memset(tab_plane[:, 1, :].bitcast(I32), 0)
        w4_plane = sbuf([P, 2, H], U8, "w4_plane")
        nc.vector.memset(w4_plane[:].rearrange("p a n -> p (a n)").bitcast(I32), 0)
        ident = sbuf([P, P], F32, "ident")
        make_identity(nc, ident[:])

        idx = load_list(offs, "idx")
        load_scale_rows(nc.scalar, tab_plane, tab_scales)
        gains = sbuf([P, 2, S], F32, "gains", tag="ring0")
        nc.sync.dma_start(gains[:, 0, :], wgs)
        table = [load_table(0)]
        w4 = [load_w4(0)]
        table.append(load_table(1))
        load_scale_rows(nc.sync, w4_plane, w4_scales)
        w1_raw = {(0, 0): load_weight(w1, 0, 0, "w1_raw00"), (0, 1): load_weight(w1, 0, 1, "w1_raw01", "late_v", 1)}
        idx2 = load_list(offs2, "idx2")
        pages = [load_page(0), load_page(1)]

        v_codes, v_scales = {}, {}

        def gather_scales(a, h, tag=None):
            v_scales[a, h] = sbuf([P, BANK], U8, "v_scales%d%d" % (a, h), tag=tag)
            nc.vector.tensor_copy(v_scales[a, h][:], tab_plane[:, a, :].indirect(idx[:, 32 * h : 32 * (h + 1)]))

        def gather_words(a, h, held):
            v_codes[a, h] = held
            nc.vector.tensor_copy(v_codes[a, h], table[a][:].indirect(idx[:, 32 * h : 32 * (h + 1)]))

        parts = sbuf([P, 2, S], F32, "gain_parts", tag="ring1")
        whole, low, mid, high = gains[:, 0, :], gains[:, 1, :], parts[:, 0, :], parts[:, 1, :]
        nc.vector.tensor_scalar(mid, whole, LN_BOTTOM, LN_TOP, ALU.max, ALU.min)
        nc.vector.tensor_scalar(low, whole, SMALLEST_NORMAL, LN_BOTTOM, ALU.max, ALU.min)
        nc.vector.tensor_scalar_max(high, whole, LN_TOP)
        first_words = sbuf([P, 2, BANK], U32, "first_words")
        gather_scales(0, 0)
        gather_scales(1, 0)
        gather_words(0, 0, first_words[:, 0, :])
        gather_words(1, 0, first_words[:, 1, :])
        gather_scales(0, 1)
        nc.scalar.activation(mid, mid, ACT.Ln)
        nc.scalar.activation(low, low, ACT.Ln, scale=LN_TOP)
        nc.scalar.activation(high, high, ACT.Ln, scale=LN_BOTTOM)
        warm = sbuf([P, 1], F32, "warm")
        nc.scalar.activation(warm[:], high[:, 0:1], ACT.Exp)
        log_banks = []

        def turn_logs(h):
            log_bank = bank("log_bank%d" % h, ("log", "stir")[h])
            for n, part in enumerate((mid, low, high)):
                for cc in range(4):
                    c = 4 * h + cc
                    nc.tensor.matmul(
                        log_bank[:, P * cc : P * (cc + 1)], part[:, P * c : P * (c + 1)], ident[:],
                        start=(n == 0 and cc == 0), stop=(n == 2 and cc == 3), is_transpose=True,
                    )
            log_banks.append(log_bank)

        turn_logs(0)
        neg_log = {0: sbuf([P, 8, P], F32, "neg_log0")[:]}

        def deal_logs(t, h):
            src = log_banks[h][:].rearrange("p (c u t) -> p c u t", c=4, t=PACK)[:, :, :, t]
            nc.scalar.activation(
                neg_log[t][:, 4 * h : 4 * h + 4, :].rearrange("p c (r u) -> p c r u", r=4),
                src.unsqueeze(2).to_broadcast([P, 4, 4, 32]),
                ACT.Copy, scale=-1.0,
            )

        size = {}

        def stir_sizes(b, h):
            tag = ("size%d" if b == 0 else "early%d") % h
            size[b, h] = sbuf([P, 4, PACK, P], F32, "size%d%d" % (b, h), tag=tag)
            for cc in range(4):
                acc = bank("stir%d%d%d" % (b, h, cc), "stir")
                cols = slice(P * cc, P * (cc + 1))
                for a in range(2):
                    nc.tensor.matmul_mx(
                        out=acc[:],
                        lhsT=v_codes[a, h][:, cols].bitcast(FP8X4), lhsT_scale=v_scales[a, h][:, cols],
                        rhs=w4[b][:, a, :].bitcast(FP4X4), rhs_scale=w4_plane[:, a, BANK * b : BANK * (b + 1)],
                        start=(a == 0), stop=(a == 1),
                    )
                nc.scalar.activation(
                    size[b, h][:, cc, :, :], acc[:].rearrange("p (q t) -> p t q", t=PACK), ACT.Abs
                )

        w1_mx = {}
        ring_tags = ["ring2", "ring0", "ring1", "last"]

        factors = {}

        def make_factors(i, h):
            b, t = divmod(i, PACK)
            cols = slice(P * t, P * (t + 1))
            if h == 0:
                factors[i] = sbuf([P, 2, S], F32, "factors%d" % i, tag=ring_tags[i % 4])
            half = slice(BANK * h, BANK * (h + 1))
            arg = bank("arg%d%d" % (i, h), "arg")
            for cc in range(4):
                nc.tensor.matmul(
                    arg[:, P * cc : P * (cc + 1)], neg_log[t][:, 4 * h + cc, :], ident[:],
                    start=(cc == 0), stop=False, is_transpose=True,
                )
            for cc in range(4):
                nc.tensor.matmul(
                    arg[:, P * cc : P * (cc + 1)], size[b, h][:, cc, t, :], ident[:],
                    start=False, stop=(cc == 3), is_transpose=True,
                )
            nc.scalar.activation(factors[i][:, 0, half], arg[:], ACT.Exp, scale=-1.0)
            level = bank("level%d%d" % (i, h), "level")
            for a in range(2):
                codes, scales = w1_mx[b, a]
                nc.tensor.matmul_mx(
                    out=level[:],
                    lhsT=codes[:, cols].bitcast(FP8X4), lhsT_scale=scales[:, cols],
                    rhs=v_codes[a, h].bitcast(FP8X4), rhs_scale=v_scales[a, h][:],
                    start=(a == 0), stop=(a == 1),
                )
            nc.scalar.copy(factors[i][:, 1, half], level[:])

        def scatter(i, first, count):
            cols = slice(first, first + count)
            nc.vector.tensor_tensor(
                pages[i][:].indirect(idx2[:, first // 16 : (first + count) // 16]),
                factors[i][:, 0, cols], factors[i][:, 1, cols], ALU.mult,
            )

        def refresh(i):
            make_factors(i, 0)
            make_factors(i, 1)
            scatter(i, 0, S)

        deal_logs(0, 0)
        stir_sizes(0, 0)
        turn_logs(1)
        rounded = round_weight(nc.vector.tensor_copy, w1_raw[0, 0], "w1_bf00", "late_scales", 1)
        w1_mx[0, 0] = quantize(rounded, "w1_00", "w1_00")
        rounded = round_weight(nc.vector.tensor_copy, w1_raw[0, 1], "w1_bf01", "late_logs", 1)
        w1_mx[0, 1] = quantize(rounded, "w1_01", "w1_01")
        second_words = sbuf([P, 2, BANK], U32, "second_words", tag="late_v")
        gather_scales(1, 1, "late_scales")
        gather_words(0, 1, second_words[:, 0, :])
        gather_words(1, 1, second_words[:, 1, :])
        late_logs = sbuf([P, 3, 8, P], F32, "late_logs")
        for t in range(1, PACK):
            neg_log[t] = late_logs[:, t - 1, :, :]
        w1_raw[1, 0] = load_weight(w1, 1, 0, "w1_raw10")
        w1_raw[1, 1] = load_weight(w1, 1, 1, "w1_raw11")
        pages.append(load_page(2))
        idx4 = load_list(offs4, "idx4")
        w4.append(load_w4(1))
        for i in range(3, 8):
            pages.append(load_page(i))
        idx3 = load_list(offs3, "idx3")
        steep_col = load_column(steep, "steep_col")
        lift_col = load_column(lift, "lift_col")
        pond_col = load_column(pond, "pond_col")
        w3_raw = [load_weight(w3, 0, a, "w3_raw0%d" % a) for a in range(2)]

        make_factors(0, 0)
        scatter(0, 0, BANK)
        stir_sizes(0, 1)
        deal_logs(0, 1)
        for i in (1, 2):
            deal_logs(i, 0)
            make_factors(i, 0)
            scatter(i, 0, BANK)
        for i in range(3):
            if i > 0:
                deal_logs(i, 1)
            make_factors(i, 1)
            scatter(i, BANK, BANK)
        w1_bf = [sbuf([P, PACK * BANK], BF16, "w1_bf1%d" % a, tag="rounded", bufs=3) for a in range(2)]
        for a in range(2):
            w1_mx[1, a] = mx_tiles("w1_1%d" % a, "w1_1%d" % a)

        def quantize_pair(u):
            for a in range(2):
                round_pairs(nc.scalar.copy, w1_bf[a], w1_raw[1, a], slice(u, u + 1))
                quantize_into(w1_mx[1, a], w1_bf[a], 2 * P * u, 2 * P)

        quantize_pair(0)
        for h in range(2):
            deal_logs(3, h)
        refresh(3)
        w3_raw.extend(load_weight(w3, 1, a, "w3_raw1%d" % a, "size%d" % a, 1) for a in range(2))
        side_early = sbuf([P, 3, M], F32, "side_early")
        for i in range(3):
            nc.vector.tensor_copy(side_early[:, i, :], pages[i][:].indirect(idx4[:]))
        for h in range(2):
            stir_sizes(1, h)
            make_factors(4, h)
            scatter(4, BANK * h, BANK)
        quantize_pair(1)
        refresh(5)
        refresh(6)
        first_picked = sbuf([P, PACK, M], F32, "first_picked", tag=ring_tags[6 % 4])
        refresh(7)
        w3_mx = {}
        for n in range(4):
            g, a = divmod(n, 2)
            place = ("rounded", 3) if n < 3 else ("early1", 1)
            rounded = round_weight(nc.scalar.copy, w3_raw[n], "w3_bf%d%d" % (g, a), *place)
            w3_mx[g, a] = quantize(rounded, "w3_%d%d" % (g, a), "w3_%d%d" % (g, a))

        x_mx = []

        def make_x(b, picked, x_bf):
            bounded = sbuf([P, PACK, M], F32, "bounded%d" % b, tag="size%d" % b)
            for t in range(PACK):
                nc.vector.tensor_copy(picked[:, t, :], pages[PACK * b + t][:].indirect(idx3[:]))
            for t in range(PACK):
                nc.scalar.activation(bounded[:, t, :], picked[:, t, :], ACT.Tanh, scale=steep_col[:, b, t : t + 1])
                nc.scalar.activation(bounded[:, t, :], bounded[:, t, :], ACT.Copy, scale=lift_col[:, b, t : t + 1])
            interleave(nc.scalar.copy, x_bf[:], bounded[:])
            x_mx.append(quantize(x_bf, "x%d" % b, "w1_0%d" % b))

        make_x(0, first_picked, sbuf([P, PACK * M], BF16, "x_bf0", tag="early0"))
        picked = sbuf([P, 5, M], F32, "picked", tag="last")
        make_x(1, picked, sbuf([P, PACK * M], BF16, "x_bf1", tag="late_x"))
        side_late = sbuf([P, 2, M], F32, "side_late", tag="late_x")
        side = [side_early[:, i, :] for i in range(3)]
        side.extend([picked[:, 4, :], picked[:, 0, :], picked[:, 1, :], side_late[:, 0, :], side_late[:, 1, :]])
        for i in range(3, 8):
            nc.vector.tensor_copy(side[i], pages[i][:].indirect(idx4[:]))

        boat_tags = [tag for tag in BANKS for n in range(BANKS[tag])]
        boats = [bank("boats%d" % i, boat_tags[i]) for i in range(8)]
        for a in range(2):
            for i in range(8):
                g, t = divmod(i, PACK)
                cols = slice(P * t, P * (t + 1))
                codes, scales = w3_mx[g, a]
                nc.tensor.matmul_mx(
                    out=boats[i][:],
                    lhsT=codes[:, cols].bitcast(FP8X4), lhsT_scale=scales[:, cols],
                    rhs=x_mx[a][0][:].bitcast(FP8X4), rhs_scale=x_mx[a][1][:],
                    start=(a == 0), stop=(a == 1),
                )

        y_codes = sbuf([P, 2, M], U32, "y_codes")
        y_scales = sbuf([P, 2, M], U8, "y_scales")
        out_rows = out_0.rearrange("(g p t) m -> g p t m", g=2, t=PACK)
        for g in range(2):
            y = sbuf([P, PACK, M], F32, "y%d" % g, tag="raw", bufs=2)
            y_bf = sbuf([P, PACK * M], BF16, "y_bf%d" % g, tag="rounded", bufs=3)
            larger = sbuf([P, PACK, M], F32, "larger%d" % g, tag="ring%d" % g)
            pieces = 1 + g
            width = M // pieces
            for n in range(pieces):
                cols = slice(width * n, width * (n + 1))
                for t in range(PACK):
                    i = PACK * g + t
                    nc.vector.scalar_tensor_tensor(
                        larger[:, t, cols], side[i][:, cols], pond_col[:, g, t : t + 1], boats[i][:, cols],
                        ALU.mult, ALU.max,
                    )
                for t in range(PACK):
                    i = PACK * g + t
                    nc.vector.tensor_tensor(y[:, t, cols], larger[:, t, cols], boats[i][:, cols], ALU.mult)
                nc.sync.dma_start(out_rows[g][:, :, cols], y[:, :, cols])
                last = g == 1 and n == pieces - 1
                wide = slice(PACK * width * n, PACK * width * (n + 1))
                interleave(nc.vector.tensor_copy if last else nc.scalar.copy, y_bf[:, wide], y[:, :, cols])
                nc.vector.quantize_mx(
                    out=y_codes[:, g, cols].bitcast(FP8X4), scales=y_scales[:, g, cols], in_=y_bf[:, wide]
                )
                words = out_1[g].rearrange("p m t -> p (m t)").bitcast(I32)
                nc.sync.dma_start(words[:, cols], y_codes[:, g, cols].bitcast(I32))
        for quad in range(QUADS):
            nc.scalar.dma_start(
                out_2[:, 4 * quad : 4 * quad + 4, :].rearrange("g r m -> r g m").bitcast(I32),
                y_scales[32 * quad : 32 * quad + 4, :, :].bitcast(I32),
            )
